import numpy as np
import ml_dtypes


def mxq(x, axis, fmt="e4m3"):
    dtype, down = {"e4m3": (ml_dtypes.float8_e4m3fn, 7), "e5m2": (ml_dtypes.float8_e5m2, 14)}[fmt]
    v = np.moveaxis(np.asarray(x, np.float32).astype(ml_dtypes.bfloat16).astype(np.float64), axis, -1)
    blocks = v.reshape(v.shape[:-1] + (-1, 32))
    amax = np.abs(blocks).max(-1, keepdims=True)
    byte = np.maximum(np.where(amax > 0, np.frexp(amax)[1] - 1 + 127, 0) - down, 1)
    scale = np.exp2(byte - 127.0)
    codes = (blocks / scale).astype(np.float32).astype(dtype).astype(np.float64)
    return np.moveaxis((codes * scale).reshape(v.shape), -1, axis)


WIDE = False


def mx_kscale(k):
    if not WIDE:
        return np.ones(k)
    levels = np.array([10, -10, 5, -5, 0])
    if k % 512:
        return np.exp2(np.random.permutation(np.resize(levels, k // 32))).repeat(32)
    a = np.empty((k // 512, 16))
    for p in range(k // 512):
        a[p, :8] = np.random.permutation(np.resize(levels, 8))
        for g in range(8):
            far = levels[np.abs(levels - a[p, g]) >= 10]
            a[p, g + 8] = far[np.random.randint(len(far))]
    return np.exp2(a.ravel()).repeat(32)


def f64(x):
    return np.asarray(x).astype(np.float64)


E2M1 = np.array([0.0, 0.5, 1.0, 1.5, 2.0, 3.0, 4.0, 6.0, -0.0, -0.5, -1.0, -1.5, -2.0, -3.0, -4.0, -6.0])


def pack_weight(w, fmt):
    k, n = w.shape
    w = f64(np.asarray(w, np.float32).astype(ml_dtypes.bfloat16)).reshape(k // 32, 32, n)
    amax = np.abs(w).max(1)
    if fmt == "e4m3":
        byte = np.frexp(amax)[1] - 1 + 127 - 7
    else:
        mant, ex = np.frexp(amax / 6.0)
        byte = np.where(mant > 0.5, ex, ex - 1) + 127
    byte = np.clip(np.where(amax > 0, byte, 1), 1, 254)
    scaled = (w * np.exp2(127.0 - byte)[:, None, :]).reshape(k, n).astype(np.float32)
    by_word = np.ascontiguousarray(scaled.reshape(k // 512, 128, 4, n).transpose(0, 1, 3, 2))
    if fmt == "e4m3":
        words = by_word.astype(ml_dtypes.float8_e4m3fn).view(np.uint8)
    else:
        c = by_word.astype(ml_dtypes.float4_e2m1fn).view(np.uint8) & 0xF
        words = (c[..., 0::2] | (c[..., 1::2] << 4)).reshape(k // 512, 128, 2 * n)
    return np.ascontiguousarray(words), np.ascontiguousarray(byte.astype(np.uint8).reshape(k // 512, 16, n))


def unpack_weight(words, scales, fmt):
    g, _, n = scales.shape
    words = np.ascontiguousarray(words).reshape(g, 128, n, -1)
    if fmt == "e4m3":
        vals = words.view(ml_dtypes.float8_e4m3fn).astype(np.float64)
    else:
        nib = np.empty((g, 128, n, 4), np.uint8)
        nib[..., 0::2] = words & 0xF
        nib[..., 1::2] = words >> 4
        vals = E2M1[nib]
    vals = vals * np.repeat(np.exp2(scales.astype(np.float64) - 127.0), 8, axis=1)[..., None]
    return vals.transpose(0, 1, 3, 2).reshape(g * 512, n)


def planes(y):
    n, m = y.shape
    v = y.astype(np.float32).astype(ml_dtypes.bfloat16).astype(np.float64).reshape(n // 32, 32, m)
    top = np.abs(v).max(1)
    byte = np.clip(np.where(top > 0, np.frexp(top)[1] - 1 + 127 - 7, 1), 1, 254)
    codes = (v * np.exp2(127.0 - byte)[:, None, :]).reshape(n, m).astype(np.float32).astype(ml_dtypes.float8_e4m3fn).view(np.uint8)
    words = codes.reshape(n // 512, 128, 4, m).transpose(0, 1, 3, 2)
    return np.ascontiguousarray(words), np.ascontiguousarray(byte.astype(np.uint8).reshape(n // 512, 16, m))


O, K, M, T = 1024, 3072, 512, 1536


def setup_inputs():
    n = np.random.standard_normal
    s = mx_kscale(K)[:, None]
    x = n((K, T)); x[:O] *= 6.0
    w = n((K, M)) / np.sqrt(K) / s; w[:O] /= 2.0
    p_w8 = pack_weight(w[:O], "e4m3")
    p_w4 = pack_weight(w[O:], "e2m1")
    return {
        "x": (x * s).astype(np.float32),
        "w8_words": p_w8[0],
        "w8_scales": p_w8[1],
        "w4_words": p_w4[0],
        "w4_scales": p_w4[1],
        "r": (n((512, 1536))).astype(np.float32),
    }


def reference(x, w8_words, w8_scales, w4_words, w4_scales, r):
    x_ = mxq(f64(x), 0, "e4m3")
    w8_ = unpack_weight(w8_words, w8_scales, "e4m3")
    w4_ = unpack_weight(w4_words, w4_scales, "e2m1")
    y = w8_.T @ x_[:O] + w4_.T @ x_[O:]
    out_0 = f64(r) + y
    return (out_0,) + planes(out_0)

@@ -1,0 +1,218 @@
+from contextlib import ExitStack
+
+import concourse.mybir as mybir
+
+O, K, M, T = 1024, 3072, 512, 1536
+FLOPS = 2 * K * M * T
+
+F32 = mybir.dt.float32
+BF16 = mybir.dt.bfloat16
+I32 = mybir.dt.int32
+U8 = mybir.dt.uint8
+FP8X4 = mybir.dt.float8_e4m3fn_x4
+FP4X4 = mybir.dt.float4_e2m1fn_x4
+
+P = 128
+PACK = 4
+K_PASS = P * PACK
+PASSES = K // K_PASS
+PASSES_FP8 = O // K_PASS
+PASSES_FP4 = PASSES - PASSES_FP8
+N = 512
+EARLY = 2 * N
+FULL = 0
+SCALES_AFTER = 2
+X_BUFS = 5
+VECTOR_COLS = 192
+VECTOR_COLS_LAST = 320
+
+
+def tile_mix_outl_fm_pl_res_kernel(
+    tc, x, w8_words, w8_scales, w4_words, w4_scales, r, out_0, out_1, out_2
+):
+    nc = tc.nc
+    with ExitStack() as ctx:
+        keep = ctx.enter_context(tc.tile_pool(name="keep", bufs=1))
+        stream = ctx.enter_context(tc.tile_pool(name="stream", bufs=X_BUFS))
+        group = ctx.enter_context(tc.tile_pool(name="group", bufs=6))
+        psum = ctx.enter_context(tc.psum_pool(name="psum", bufs=1))
+        ctx.enter_context(tc.manual_schedule())
+
+        w8_raw = keep.tile([P, PASSES_FP8, M], I32, align_bytes=64)
+        w8 = keep.tile([P, PASSES_FP8, M], I32, align_bytes=64)
+        w4_raw = keep.tile([P, PASSES_FP4, 2 * M], U8, align_bytes=64)
+        w4 = keep.tile([P, PASSES_FP4, 2 * M], U8, align_bytes=64)
+        ws_raw = keep.tile([P, PASSES, M], U8, align_bytes=64)
+        ws = keep.tile([P, PASSES, M], U8, align_bytes=64)
+        x_codes = keep.tile([P, PASSES, T], I32, align_bytes=64)
+        x_scales = keep.tile([P, PASSES, T], U8, align_bytes=64)
+        y_early = keep.tile([P, PACK, EARLY], F32, align_bytes=64)
+        y_late = keep.tile([P, PACK, T - EARLY], F32, align_bytes=64)
+        y_codes = keep.tile([P, T], I32, align_bytes=64)
+        y_scales = keep.tile([P, T], U8, align_bytes=64)
+
+        r_rows = r.rearrange("(p i) t -> p i t", i=PACK)
+        out_rows = out_0.rearrange("(p i) t -> p i t", i=PACK)
+        out_words = out_1[0].rearrange("p t i -> p (t i)").bitcast(I32)
+
+        x_loads = [(g, 0, T if g < FULL else EARLY) for g in range(PASSES)]
+        x_loads += [(g, EARLY, T) for g in range(FULL, PASSES)]
+        x_raw = {}
+
+        def load_x(k):
+            if k == PASSES:
+                nc.sync.dma_start(out=y_early[:], in_=r_rows[:, :, 0:EARLY])
+            if k == len(x_loads):
+                nc.sync.dma_start(out=y_late[:], in_=r_rows[:, :, EARLY:T])
+            if k >= len(x_loads):
+                return
+            g, t0, t1 = x_loads[k]
+            raw = stream.tile([P, PACK, t1 - t0], F32, name="raw", tag="raw", align_bytes=64)
+            rows = x[g * K_PASS : (g + 1) * K_PASS, :].rearrange("(p j) t -> p j t", j=PACK)
+            nc.sync.dma_start(out=raw[:], in_=rows[:, :, t0:t1])
+            x_raw[k] = raw
+
+        def interleave(src, vector_cols):
+            grouped = group.tile([P, N, PACK], BF16, name="grouped", tag="grouped", align_bytes=64)
+            nc.vector.tensor_copy(
+                out=grouped[:, 0:vector_cols, :].rearrange("p (c i) j -> p c j i", i=4),
+                in_=src[:, :, 0:vector_cols].rearrange("p j (c i) -> p c j i", i=4),
+            )
+            nc.scalar.copy(
+                out=grouped[:, vector_cols:N, :].rearrange("p (c i) j -> p c j i", i=4),
+                in_=src[:, :, vector_cols:N].rearrange("p j (c i) -> p c j i", i=4),
+            )
+            return grouped
+
+        def quantize(grouped, codes, scales):
+            nc.vector.quantize_mx(
+                out=codes.bitcast(FP8X4),
+                scales=scales,
+                in_=grouped[:].rearrange("p c j -> p (c j)"),
+            )
+
+        acc = {}
+
+        def multiply(g, c):
+            cols = slice(c * N, (c + 1) * N)
+            for i in range(PACK):
+                if g == 0:
+                    bank = "bank%d" % ((c % 2) * PACK + i)
+                    acc[c, i] = psum.tile([P, N], F32, name=bank, tag=bank)
+                if g < PASSES_FP8:
+                    weights = w8[:, g, i * P : (i + 1) * P].bitcast(FP8X4)
+                else:
+                    weights = w4[:, g - PASSES_FP8, 2 * i * P : 2 * (i + 1) * P].bitcast(FP4X4)
+                nc.tensor.matmul_mx(
+                    out=acc[c, i][:],
+                    lhsT=weights,
+                    lhsT_scale=ws[:, g, i * P : (i + 1) * P],
+                    rhs=x_codes[:, g, cols].bitcast(FP8X4),
+                    rhs_scale=x_scales[:, g, cols],
+                    start=(g == 0),
+                    stop=(g == PASSES - 1),
+                )
+
+        def y_chunk(c):
+            if c * N < EARLY:
+                return y_early[:, :, c * N : (c + 1) * N]
+            return y_late[:]
+
+        def add_residual(c, tiles):
+            for i in tiles:
+                y = y_chunk(c)[:, i, :]
+                nc.vector.tensor_tensor(out=y, in0=acc[c, i][:], in1=y, op=mybir.AluOpType.add)
+
+        def quantize_y(grouped, c):
+            cols = slice(c * N, (c + 1) * N)
+            quantize(grouped, y_codes[:, cols], y_scales[:, cols])
+
+        nc.gpsimd.memset(ws_raw[:].rearrange("p g n -> p (g n)").bitcast(I32), 0)
+        for q in range(4):
+            rows = slice(4 * q, 4 * q + 4)
+            parts = slice(32 * q, 32 * q + 4)
+            nc.gpsimd.dma_start(
+                out=ws_raw[parts, 0:PASSES_FP8, :].bitcast(I32),
+                in_=w8_scales[:, rows, :].rearrange("g q n -> q g n").bitcast(I32),
+            )
+            nc.gpsimd.dma_start(
+                out=ws_raw[parts, PASSES_FP8:PASSES, :].bitcast(I32),
+                in_=w4_scales[:, rows, :].rearrange("g q n -> q g n").bitcast(I32),
+            )
+
+        nc.sync.dma_start(out=w8_raw[:], in_=w8_words.rearrange("g p n i -> p g (n i)").bitcast(I32))
+        nc.sync.dma_start(out=w4_raw[:].bitcast(I32), in_=w4_words.rearrange("g p b -> p g b").bitcast(I32))
+        for k in range(X_BUFS):
+            load_x(k)
+
+        nc.vector.tensor_copy(
+            out=w8[:].rearrange("p g (i m) -> p g i m", i=PACK),
+            in_=w8_raw[:].rearrange("p g (m i) -> p g i m", i=PACK),
+        )
+        for g in range(PASSES_FP4):
+            nc.vector.tensor_copy(
+                out=w4[:, g, :].rearrange("p (i m b) -> p i m b", i=PACK, b=2),
+                in_=w4_raw[:, g, :].rearrange("p (m i b) -> p i m b", i=PACK, b=2),
+            )
+
+        for k in range(PASSES):
+            g, t0, t1 = x_loads[k]
+            chunks = range(t0 // N, t1 // N)
+            grouped = [interleave(x_raw[k][:, :, c * N : (c + 1) * N], VECTOR_COLS) for c in chunks]
+            load_x(k + X_BUFS)
+            for c in chunks:
+                quantize(grouped[c], x_codes[:, g, c * N : (c + 1) * N], x_scales[:, g, c * N : (c + 1) * N])
+            if k == SCALES_AFTER:
+                nc.vector.tensor_copy(
+                    out=ws[:].rearrange("p g (i m) -> p g i m", i=PACK),
+                    in_=ws_raw[:].rearrange("p g (m i) -> p g i m", i=PACK),
+                )
+            if k >= SCALES_AFTER:
+                for h in range(0 if k == SCALES_AFTER else g, g + 1):
+                    for c in range(2):
+                        multiply(h, c)
+
+        y_grouped = {}
+
+        def filler(step):
+            if step == "add1a":
+                add_residual(1, [0, 1])
+            if step == "add1b":
+                add_residual(1, [2, 3])
+            if step == "cast0":
+                y_grouped[0] = interleave(y_chunk(0), VECTOR_COLS)
+            if step == "cast1":
+                y_grouped[1] = interleave(y_chunk(1), VECTOR_COLS)
+            if step == "quant0":
+                quantize_y(y_grouped[0], 0)
+            if step == "quant1":
+                quantize_y(y_grouped[1], 1)
+
+        fillers = [["add1a"], ["add1b"], ["cast0"], ["quant0", "cast1"], ["quant1"], [], []]
+        add_residual(0, range(PACK))
+        for g in range(FULL):
+            multiply(g, 2)
+        late = slice(EARLY, T)
+        for k in range(PASSES, len(x_loads)):
+            g = x_loads[k][0]
+            last = k == len(x_loads) - 1
+            grouped = interleave(x_raw[k][:], VECTOR_COLS_LAST if last else VECTOR_COLS)
+            load_x(k + X_BUFS)
+            for step in fillers[k - PASSES]:
+                filler(step)
+            quantize(grouped, x_codes[:, g, late], x_scales[:, g, late])
+            multiply(g, 2)
+        for step in fillers[-1]:
+            filler(step)
+
+        nc.sync.dma_start(out=out_rows[:, :, 0:EARLY], in_=y_early[:])
+        nc.sync.dma_start(out=out_words[:, 0:EARLY], in_=y_codes[:, 0:EARLY])
+        add_residual(2, range(PACK))
+        nc.sync.dma_start(out=out_rows[:, :, EARLY:T], in_=y_late[:])
+        quantize_y(interleave(y_late[:], VECTOR_COLS_LAST), 2)
+        nc.sync.dma_start(out=out_words[:, EARLY:T], in_=y_codes[:, EARLY:T])
+        for q in range(4):
+            nc.scalar.dma_start(
+                out=out_2[0, 4 * q : 4 * q + 4, :].bitcast(I32),
+                in_=y_scales[32 * q : 32 * q + 4, :].bitcast(I32),
+            )

@@ -19,12 +19,14 @@ PASSES = K // K_PASS
 PASSES_FP8 = O // K_PASS
 PASSES_FP4 = PASSES - PASSES_FP8
 N = 512
+X_BUFS = 4
+VECTOR_COLS = 256
+CHUNKS = T // N
+SCALES_AFTER = 1
+LAST = PASSES - 1
+FULL = 3
 EARLY = 2 * N
-FULL = 0
-SCALES_AFTER = 2
-X_BUFS = 5
-VECTOR_COLS = 192
-VECTOR_COLS_LAST = 320
+VA, VB, Y0, Y1, Y2 = 320, 320, 0, 256, 256
 
 
 def tile_mix_outl_fm_pl_res_kernel(
@@ -55,14 +57,21 @@ def tile_mix_outl_fm_pl_res_kernel(
         out_rows = out_0.rearrange("(p i) t -> p i t", i=PACK)
         out_words = out_1[0].rearrange("p t i -> p (t i)").bitcast(I32)
 
+        def chunk(c):
+            return slice(c * N, (c + 1) * N)
+
+        def y_chunk(c):
+            return y_early[:, :, chunk(c)] if c < 2 else y_late[:]
+
         x_loads = [(g, 0, T if g < FULL else EARLY) for g in range(PASSES)]
         x_loads += [(g, EARLY, T) for g in range(FULL, PASSES)]
         x_raw = {}
 
         def load_x(k):
             if k == PASSES:
-                nc.sync.dma_start(out=y_early[:], in_=r_rows[:, :, 0:EARLY])
+                nc.sync.dma_start(out=y_early[:, 0:2, :], in_=r_rows[:, 0:2, 0:EARLY])
             if k == len(x_loads):
+                nc.sync.dma_start(out=y_early[:, 2:4, :], in_=r_rows[:, 2:4, 0:EARLY])
                 nc.sync.dma_start(out=y_late[:], in_=r_rows[:, :, EARLY:T])
             if k >= len(x_loads):
                 return
@@ -74,14 +83,16 @@ def tile_mix_outl_fm_pl_res_kernel(
 
         def interleave(src, vector_cols):
             grouped = group.tile([P, N, PACK], BF16, name="grouped", tag="grouped", align_bytes=64)
-            nc.vector.tensor_copy(
-                out=grouped[:, 0:vector_cols, :].rearrange("p (c i) j -> p c j i", i=4),
-                in_=src[:, :, 0:vector_cols].rearrange("p j (c i) -> p c j i", i=4),
-            )
-            nc.scalar.copy(
-                out=grouped[:, vector_cols:N, :].rearrange("p (c i) j -> p c j i", i=4),
-                in_=src[:, :, vector_cols:N].rearrange("p j (c i) -> p c j i", i=4),
-            )
+            if vector_cols > 0:
+                nc.vector.tensor_copy(
+                    out=grouped[:, 0:vector_cols, :].rearrange("p (c i) j -> p c j i", i=4),
+                    in_=src[:, :, 0:vector_cols].rearrange("p j (c i) -> p c j i", i=4),
+                )
+            if vector_cols < N:
+                nc.scalar.copy(
+                    out=grouped[:, vector_cols:N, :].rearrange("p (c i) j -> p c j i", i=4),
+                    in_=src[:, :, vector_cols:N].rearrange("p j (c i) -> p c j i", i=4),
+                )
             return grouped
 
         def quantize(grouped, codes, scales):
@@ -91,41 +102,47 @@ def tile_mix_outl_fm_pl_res_kernel(
                 in_=grouped[:].rearrange("p c j -> p (c j)"),
             )
 
+        def quantize_x(grouped, g, c):
+            quantize(grouped, x_codes[:, g, chunk(c)], x_scales[:, g, chunk(c)])
+
+        def quantize_y(grouped, c):
+            quantize(grouped, y_codes[:, chunk(c)], y_scales[:, chunk(c)])
+
+        bank_of = {(i, c): c * PACK + i for c in range(2) for i in range(PACK)}
+        for i in range(PACK):
+            bank_of[i, 2] = bank_of[i % 2, i // 2]
         acc = {}
 
-        def multiply(g, c):
-            cols = slice(c * N, (c + 1) * N)
-            for i in range(PACK):
+        def multiply(i, c, passes):
+            for g in passes:
                 if g == 0:
-                    bank = "bank%d" % ((c % 2) * PACK + i)
-                    acc[c, i] = psum.tile([P, N], F32, name=bank, tag=bank)
+                    bank = "bank%d" % bank_of[i, c]
+                    acc[i, c] = psum.tile([P, N], F32, name=bank, tag=bank)
                 if g < PASSES_FP8:
                     weights = w8[:, g, i * P : (i + 1) * P].bitcast(FP8X4)
                 else:
                     weights = w4[:, g - PASSES_FP8, 2 * i * P : 2 * (i + 1) * P].bitcast(FP4X4)
                 nc.tensor.matmul_mx(
-                    out=acc[c, i][:],
+                    out=acc[i, c][:],
                     lhsT=weights,
                     lhsT_scale=ws[:, g, i * P : (i + 1) * P],
-                    rhs=x_codes[:, g, cols].bitcast(FP8X4),
-                    rhs_scale=x_scales[:, g, cols],
+                    rhs=x_codes[:, g, chunk(c)].bitcast(FP8X4),
+                    rhs_scale=x_scales[:, g, chunk(c)],
                     start=(g == 0),
-                    stop=(g == PASSES - 1),
+                    stop=(g == LAST),
                 )
 
-        def y_chunk(c):
-            if c * N < EARLY:
-                return y_early[:, :, c * N : (c + 1) * N]
-            return y_late[:]
+        def multiply_chunk(g, c):
+            for i in range(PACK):
+                multiply(i, c, [g])
 
-        def add_residual(c, tiles):
-            for i in tiles:
-                y = y_chunk(c)[:, i, :]
-                nc.vector.tensor_tensor(out=y, in0=acc[c, i][:], in1=y, op=mybir.AluOpType.add)
+        def add_residual(i, c):
+            nc.vector.tensor_tensor(
+                out=y_chunk(c)[:, i, :], in0=acc[i, c][:], in1=y_chunk(c)[:, i, :], op=mybir.AluOpType.add
+            )
 
-        def quantize_y(grouped, c):
-            cols = slice(c * N, (c + 1) * N)
-            quantize(grouped, y_codes[:, cols], y_scales[:, cols])
+        def store_y(src, i0, i1, t0, t1):
+            nc.sync.dma_start(out=out_rows[:, i0:i1, t0:t1], in_=src[:, i0:i1, :])
 
         nc.gpsimd.memset(ws_raw[:].rearrange("p g n -> p (g n)").bitcast(I32), 0)
         for q in range(4):
@@ -155,62 +172,57 @@ def tile_mix_outl_fm_pl_res_kernel(
                 in_=w4_raw[:, g, :].rearrange("p (m i b) -> p i m b", i=PACK, b=2),
             )
 
-        for k in range(PASSES):
-            g, t0, t1 = x_loads[k]
-            chunks = range(t0 // N, t1 // N)
-            grouped = [interleave(x_raw[k][:, :, c * N : (c + 1) * N], VECTOR_COLS) for c in chunks]
-            load_x(k + X_BUFS)
-            for c in chunks:
-                quantize(grouped[c], x_codes[:, g, c * N : (c + 1) * N], x_scales[:, g, c * N : (c + 1) * N])
-            if k == SCALES_AFTER:
+        for g in range(FULL):
+            grouped = [interleave(x_raw[g][:, :, chunk(c)], VECTOR_COLS) for c in range(CHUNKS)]
+            load_x(g + X_BUFS)
+            for c in range(CHUNKS):
+                quantize_x(grouped[c], g, c)
+            if g == SCALES_AFTER:
                 nc.vector.tensor_copy(
                     out=ws[:].rearrange("p g (i m) -> p g i m", i=PACK),
                     in_=ws_raw[:].rearrange("p g (m i) -> p g i m", i=PACK),
                 )
-            if k >= SCALES_AFTER:
-                for h in range(0 if k == SCALES_AFTER else g, g + 1):
+            if g >= SCALES_AFTER:
+                for h in range(0 if g == SCALES_AFTER else g, g + 1):
                     for c in range(2):
-                        multiply(h, c)
+                        multiply_chunk(h, c)
 
-        y_grouped = {}
+        for g in range(FULL, PASSES):
+            grouped = [interleave(x_raw[g][:, :, chunk(c)], VA) for c in range(2)]
+            load_x(g + X_BUFS)
+            for c in range(2):
+                quantize_x(grouped[c], g, c)
+                multiply_chunk(g, c)
 
-        def filler(step):
-            if step == "add1a":
-                add_residual(1, [0, 1])
-            if step == "add1b":
-                add_residual(1, [2, 3])
-            if step == "cast0":
-                y_grouped[0] = interleave(y_chunk(0), VECTOR_COLS)
-            if step == "cast1":
-                y_grouped[1] = interleave(y_chunk(1), VECTOR_COLS)
-            if step == "quant0":
-                quantize_y(y_grouped[0], 0)
-            if step == "quant1":
-                quantize_y(y_grouped[1], 1)
-
-        fillers = [["add1a"], ["add1b"], ["cast0"], ["quant0", "cast1"], ["quant1"], [], []]
-        add_residual(0, range(PACK))
-        for g in range(FULL):
-            multiply(g, 2)
-        late = slice(EARLY, T)
+        add_residual(0, 0)
+        add_residual(1, 0)
         for k in range(PASSES, len(x_loads)):
             g = x_loads[k][0]
-            last = k == len(x_loads) - 1
-            grouped = interleave(x_raw[k][:], VECTOR_COLS_LAST if last else VECTOR_COLS)
+            grouped = interleave(x_raw[k][:], VB)
             load_x(k + X_BUFS)
-            for step in fillers[k - PASSES]:
-                filler(step)
-            quantize(grouped, x_codes[:, g, late], x_scales[:, g, late])
-            multiply(g, 2)
-        for step in fillers[-1]:
-            filler(step)
-
-        nc.sync.dma_start(out=out_rows[:, :, 0:EARLY], in_=y_early[:])
-        nc.sync.dma_start(out=out_words[:, 0:EARLY], in_=y_codes[:, 0:EARLY])
-        add_residual(2, range(PACK))
-        nc.sync.dma_start(out=out_rows[:, :, EARLY:T], in_=y_late[:])
-        quantize_y(interleave(y_late[:], VECTOR_COLS_LAST), 2)
-        nc.sync.dma_start(out=out_words[:, EARLY:T], in_=y_codes[:, EARLY:T])
+            if g == FULL:
+                add_residual(0, 1)
+                add_residual(1, 1)
+                for h in range(FULL):
+                    multiply_chunk(h, 2)
+            quantize_x(grouped, g, 2)
+            multiply_chunk(g, 2)
+        store_y(y_early, 0, 2, 0, EARLY)
+        add_residual(2, 1)
+        add_residual(2, 0)
+        add_residual(3, 0)
+        grouped_0 = interleave(y_chunk(0), Y0)
+        add_residual(3, 1)
+        store_y(y_early, 2, 4, 0, EARLY)
+        for i in range(PACK):
+            add_residual(i, 2)
+        store_y(y_late, 0, 4, EARLY, T)
+        grouped_1 = interleave(y_chunk(1), Y1)
+        quantize_y(grouped_0, 0)
+        quantize_y(grouped_1, 1)
+        nc.sync.dma_start(out=out_words[:, 0 : 2 * N], in_=y_codes[:, 0 : 2 * N])
+        quantize_y(interleave(y_chunk(2), Y2), 2)
+        nc.sync.dma_start(out=out_words[:, 2 * N : T], in_=y_codes[:, 2 * N : T])
         for q in range(4):
             nc.scalar.dma_start(
                 out=out_2[0, 4 * q : 4 * q + 4, :].bitcast(I32),

@@ -26,7 +26,7 @@ SCALES_AFTER = 1
 LAST = PASSES - 1
 FULL = 3
 EARLY = 2 * N
-VA, VB, Y0, Y1, Y2 = 320, 320, 0, 256, 256
+VA, VB, Y0, Y1, Y2 = 256, 224, 0, 192, 224
 
 
 def tile_mix_outl_fm_pl_res_kernel(
@@ -85,13 +85,13 @@ def tile_mix_outl_fm_pl_res_kernel(
             grouped = group.tile([P, N, PACK], BF16, name="grouped", tag="grouped", align_bytes=64)
             if vector_cols > 0:
                 nc.vector.tensor_copy(
-                    out=grouped[:, 0:vector_cols, :].rearrange("p (c i) j -> p c j i", i=4),
-                    in_=src[:, :, 0:vector_cols].rearrange("p j (c i) -> p c j i", i=4),
+                    out=grouped[:, 0:vector_cols, :].rearrange("p (c i) j -> p c j i", i=2),
+                    in_=src[:, :, 0:vector_cols].rearrange("p j (c i) -> p c j i", i=2),
                 )
             if vector_cols < N:
                 nc.scalar.copy(
-                    out=grouped[:, vector_cols:N, :].rearrange("p (c i) j -> p c j i", i=4),
-                    in_=src[:, :, vector_cols:N].rearrange("p j (c i) -> p c j i", i=4),
+                    out=grouped[:, vector_cols:N, :].rearrange("p (c i) j -> p c j i", i=2),
+                    in_=src[:, :, vector_cols:N].rearrange("p j (c i) -> p c j i", i=2),
                 )
             return grouped
 

from contextlib import ExitStack

import concourse.mybir as mybir

O, K, M, T = 1024, 3072, 512, 1536
FLOPS = 2 * K * M * T

F32 = mybir.dt.float32
BF16 = mybir.dt.bfloat16
I32 = mybir.dt.int32
U8 = mybir.dt.uint8
FP8X4 = mybir.dt.float8_e4m3fn_x4
FP4X4 = mybir.dt.float4_e2m1fn_x4

P = 128
PACK = 4
K_PASS = P * PACK
PASSES = K // K_PASS
PASSES_FP8 = O // K_PASS
PASSES_FP4 = PASSES - PASSES_FP8
N = 512
X_BUFS = 4
VECTOR_COLS = 256
CHUNKS = T // N
SCALES_AFTER = 1
LAST = PASSES - 1
FULL = 3
EARLY = 2 * N
VA, VB, Y0, Y1, Y2 = 256, 224, 0, 192, 224


def tile_mix_outl_fm_pl_res_kernel(
    tc, x, w8_words, w8_scales, w4_words, w4_scales, r, out_0, out_1, out_2
):
    nc = tc.nc
    with ExitStack() as ctx:
        keep = ctx.enter_context(tc.tile_pool(name="keep", bufs=1))
        stream = ctx.enter_context(tc.tile_pool(name="stream", bufs=X_BUFS))
        group = ctx.enter_context(tc.tile_pool(name="group", bufs=6))
        psum = ctx.enter_context(tc.psum_pool(name="psum", bufs=1))
        ctx.enter_context(tc.manual_schedule())

        w8_raw = keep.tile([P, PASSES_FP8, M], I32, align_bytes=64)
        w8 = keep.tile([P, PASSES_FP8, M], I32, align_bytes=64)
        w4_raw = keep.tile([P, PASSES_FP4, 2 * M], U8, align_bytes=64)
        w4 = keep.tile([P, PASSES_FP4, 2 * M], U8, align_bytes=64)
        ws_raw = keep.tile([P, PASSES, M], U8, align_bytes=64)
        ws = keep.tile([P, PASSES, M], U8, align_bytes=64)
        x_codes = keep.tile([P, PASSES, T], I32, align_bytes=64)
        x_scales = keep.tile([P, PASSES, T], U8, align_bytes=64)
        y_early = keep.tile([P, PACK, EARLY], F32, align_bytes=64)
        y_late = keep.tile([P, PACK, T - EARLY], F32, align_bytes=64)
        y_codes = keep.tile([P, T], I32, align_bytes=64)
        y_scales = keep.tile([P, T], U8, align_bytes=64)

        r_rows = r.rearrange("(p i) t -> p i t", i=PACK)
        out_rows = out_0.rearrange("(p i) t -> p i t", i=PACK)
        out_words = out_1[0].rearrange("p t i -> p (t i)").bitcast(I32)

        def chunk(c):
            return slice(c * N, (c + 1) * N)

        def y_chunk(c):
            return y_early[:, :, chunk(c)] if c < 2 else y_late[:]

        x_loads = [(g, 0, T if g < FULL else EARLY) for g in range(PASSES)]
        x_loads += [(g, EARLY, T) for g in range(FULL, PASSES)]
        x_raw = {}

        def load_x(k):
            if k == PASSES:
                nc.sync.dma_start(out=y_early[:, 0:2, :], in_=r_rows[:, 0:2, 0:EARLY])
            if k == len(x_loads):
                nc.sync.dma_start(out=y_early[:, 2:4, :], in_=r_rows[:, 2:4, 0:EARLY])
                nc.sync.dma_start(out=y_late[:], in_=r_rows[:, :, EARLY:T])
            if k >= len(x_loads):
                return
            g, t0, t1 = x_loads[k]
            raw = stream.tile([P, PACK, t1 - t0], F32, name="raw", tag="raw", align_bytes=64)
            rows = x[g * K_PASS : (g + 1) * K_PASS, :].rearrange("(p j) t -> p j t", j=PACK)
            nc.sync.dma_start(out=raw[:], in_=rows[:, :, t0:t1])
            x_raw[k] = raw

        def interleave(src, vector_cols):
            grouped = group.tile([P, N, PACK], BF16, name="grouped", tag="grouped", align_bytes=64)
            if vector_cols > 0:
                nc.vector.tensor_copy(
                    out=grouped[:, 0:vector_cols, :].rearrange("p (c i) j -> p c j i", i=2),
                    in_=src[:, :, 0:vector_cols].rearrange("p j (c i) -> p c j i", i=2),
                )
            if vector_cols < N:
                nc.scalar.copy(
                    out=grouped[:, vector_cols:N, :].rearrange("p (c i) j -> p c j i", i=2),
                    in_=src[:, :, vector_cols:N].rearrange("p j (c i) -> p c j i", i=2),
                )
            return grouped

        def quantize(grouped, codes, scales):
            nc.vector.quantize_mx(
                out=codes.bitcast(FP8X4),
                scales=scales,
                in_=grouped[:].rearrange("p c j -> p (c j)"),
            )

        def quantize_x(grouped, g, c):
            quantize(grouped, x_codes[:, g, chunk(c)], x_scales[:, g, chunk(c)])

        def quantize_y(grouped, c):
            quantize(grouped, y_codes[:, chunk(c)], y_scales[:, chunk(c)])

        bank_of = {(i, c): c * PACK + i for c in range(2) for i in range(PACK)}
        for i in range(PACK):
            bank_of[i, 2] = bank_of[i % 2, i // 2]
        acc = {}

        def multiply(i, c, passes):
            for g in passes:
                if g == 0:
                    bank = "bank%d" % bank_of[i, c]
                    acc[i, c] = psum.tile([P, N], F32, name=bank, tag=bank)
                if g < PASSES_FP8:
                    weights = w8[:, g, i * P : (i + 1) * P].bitcast(FP8X4)
                else:
                    weights = w4[:, g - PASSES_FP8, 2 * i * P : 2 * (i + 1) * P].bitcast(FP4X4)
                nc.tensor.matmul_mx(
                    out=acc[i, c][:],
                    lhsT=weights,
                    lhsT_scale=ws[:, g, i * P : (i + 1) * P],
                    rhs=x_codes[:, g, chunk(c)].bitcast(FP8X4),
                    rhs_scale=x_scales[:, g, chunk(c)],
                    start=(g == 0),
                    stop=(g == LAST),
                )

        def multiply_chunk(g, c):
            for i in range(PACK):
                multiply(i, c, [g])

        def add_residual(i, c):
            nc.vector.tensor_tensor(
                out=y_chunk(c)[:, i, :], in0=acc[i, c][:], in1=y_chunk(c)[:, i, :], op=mybir.AluOpType.add
            )

        def store_y(src, i0, i1, t0, t1):
            nc.sync.dma_start(out=out_rows[:, i0:i1, t0:t1], in_=src[:, i0:i1, :])

        nc.gpsimd.memset(ws_raw[:].rearrange("p g n -> p (g n)").bitcast(I32), 0)
        for q in range(4):
            rows = slice(4 * q, 4 * q + 4)
            parts = slice(32 * q, 32 * q + 4)
            nc.gpsimd.dma_start(
                out=ws_raw[parts, 0:PASSES_FP8, :].bitcast(I32),
                in_=w8_scales[:, rows, :].rearrange("g q n -> q g n").bitcast(I32),
            )
            nc.gpsimd.dma_start(
                out=ws_raw[parts, PASSES_FP8:PASSES, :].bitcast(I32),
                in_=w4_scales[:, rows, :].rearrange("g q n -> q g n").bitcast(I32),
            )

        nc.sync.dma_start(out=w8_raw[:], in_=w8_words.rearrange("g p n i -> p g (n i)").bitcast(I32))
        nc.sync.dma_start(out=w4_raw[:].bitcast(I32), in_=w4_words.rearrange("g p b -> p g b").bitcast(I32))
        for k in range(X_BUFS):
            load_x(k)

        nc.vector.tensor_copy(
            out=w8[:].rearrange("p g (i m) -> p g i m", i=PACK),
            in_=w8_raw[:].rearrange("p g (m i) -> p g i m", i=PACK),
        )
        for g in range(PASSES_FP4):
            nc.vector.tensor_copy(
                out=w4[:, g, :].rearrange("p (i m b) -> p i m b", i=PACK, b=2),
                in_=w4_raw[:, g, :].rearrange("p (m i b) -> p i m b", i=PACK, b=2),
            )

        for g in range(FULL):
            grouped = [interleave(x_raw[g][:, :, chunk(c)], VECTOR_COLS) for c in range(CHUNKS)]
            load_x(g + X_BUFS)
            for c in range(CHUNKS):
                quantize_x(grouped[c], g, c)
            if g == SCALES_AFTER:
                nc.vector.tensor_copy(
                    out=ws[:].rearrange("p g (i m) -> p g i m", i=PACK),
                    in_=ws_raw[:].rearrange("p g (m i) -> p g i m", i=PACK),
                )
            if g >= SCALES_AFTER:
                for h in range(0 if g == SCALES_AFTER else g, g + 1):
                    for c in range(2):
                        multiply_chunk(h, c)

        for g in range(FULL, PASSES):
            grouped = [interleave(x_raw[g][:, :, chunk(c)], VA) for c in range(2)]
            load_x(g + X_BUFS)
            for c in range(2):
                quantize_x(grouped[c], g, c)
                multiply_chunk(g, c)

        add_residual(0, 0)
        add_residual(1, 0)
        for k in range(PASSES, len(x_loads)):
            g = x_loads[k][0]
            grouped = interleave(x_raw[k][:], VB)
            load_x(k + X_BUFS)
            if g == FULL:
                add_residual(0, 1)
                add_residual(1, 1)
                for h in range(FULL):
                    multiply_chunk(h, 2)
            quantize_x(grouped, g, 2)
            multiply_chunk(g, 2)
        store_y(y_early, 0, 2, 0, EARLY)
        add_residual(2, 1)
        add_residual(2, 0)
        add_residual(3, 0)
        grouped_0 = interleave(y_chunk(0), Y0)
        add_residual(3, 1)
        store_y(y_early, 2, 4, 0, EARLY)
        for i in range(PACK):
            add_residual(i, 2)
        store_y(y_late, 0, 4, EARLY, T)
        grouped_1 = interleave(y_chunk(1), Y1)
        quantize_y(grouped_0, 0)
        quantize_y(grouped_1, 1)
        nc.sync.dma_start(out=out_words[:, 0 : 2 * N], in_=y_codes[:, 0 : 2 * N])
        quantize_y(interleave(y_chunk(2), Y2), 2)
        nc.sync.dma_start(out=out_words[:, 2 * N : T], in_=y_codes[:, 2 * N : T])
        for q in range(4):
            nc.scalar.dma_start(
                out=out_2[0, 4 * q : 4 * q + 4, :].bitcast(I32),
                in_=y_scales[32 * q : 32 * q + 4, :].bitcast(I32),
            )
